import numpy as np
import ml_dtypes


def mxq(x, axis, fmt="e4m3"):
    dtype, down = {"e4m3": (ml_dtypes.float8_e4m3fn, 7), "e5m2": (ml_dtypes.float8_e5m2, 14)}[fmt]
    v = np.moveaxis(np.asarray(x, np.float32).astype(ml_dtypes.bfloat16).astype(np.float64), axis, -1)
    blocks = v.reshape(v.shape[:-1] + (-1, 32))
    amax = np.abs(blocks).max(-1, keepdims=True)
    byte = np.maximum(np.where(amax > 0, np.frexp(amax)[1] - 1 + 127, 0) - down, 1)
    scale = np.exp2(byte - 127.0)
    codes = (blocks / scale).astype(np.float32).astype(dtype).astype(np.float64)
    return np.moveaxis((codes * scale).reshape(v.shape), -1, axis)


WIDE = False


def mx_kscale(k):
    if not WIDE:
        return np.ones(k)
    levels = np.array([10, -10, 5, -5, 0])
    if k % 512:
        return np.exp2(np.random.permutation(np.resize(levels, k // 32))).repeat(32)
    a = np.empty((k // 512, 16))
    for p in range(k // 512):
        a[p, :8] = np.random.permutation(np.resize(levels, 8))
        for g in range(8):
            far = levels[np.abs(levels - a[p, g]) >= 10]
            a[p, g + 8] = far[np.random.randint(len(far))]
    return np.exp2(a.ravel()).repeat(32)


def f64(x):
    return np.asarray(x).astype(np.float64)


def striped(idx):
    return np.tile(idx.reshape(-1, 16).T, (8, 1)).astype(np.uint16)


def unstriped(offs):
    return offs[:16].T.reshape(-1).astype(np.int64)


K, T, E, C, N = 1024, 512, 6, 256, 256
TOP = 3
M = 1024


def by_expert(wq, xq):
    return np.concatenate([wq[e].T @ xq[:, e * C:(e + 1) * C] for e in range(E)], axis=1)


def setup_inputs():
    n = np.random.standard_normal
    s = mx_kscale(K)[:, None]
    deal = np.repeat(np.arange(E), C).reshape(TOP, T)[:, np.random.permutation(T)]
    deal = np.take_along_axis(deal, np.argsort(np.random.rand(TOP, T), axis=0), axis=0)
    for _ in range(8):
        s_, t_ = np.random.permutation(T).reshape(2, -1); r = np.random.randint(TOP, size=T // 2); x, y = deal[r, s_].copy(), deal[r, t_].copy()
        ok = ~((deal[:, s_] == y).any(0) | (deal[:, t_] == x).any(0)); deal[r[ok], s_[ok]] = y[ok]; deal[r[ok], t_[ok]] = x[ok]
    order = np.lexsort((np.random.rand(TOP * T), deal.reshape(-1)))
    slot_token = order % T; pos = np.empty(TOP * T, np.int64); pos[order] = np.arange(TOP * T); pos = pos.reshape(TOP, T)
    g = np.random.uniform(0.5, 1.5, (TOP, T)); g = g / g.sum(0)
    r = mx_kscale(M)[:, None]
    return {
        "uT": (n((M, T)) * r).astype(np.float32),
        "wu": (n((M, K)) / np.sqrt(M) / r * s.T).astype(np.float32),
        "w": (n((E, K, N)) / np.sqrt(K) / s[None]).astype(np.float32),
        "b": (0.3 * n((N, E))).astype(np.float32),
        "gate": np.stack([np.tile(r, (N, 1)) for r in g]).astype(np.float32),
        "offs": striped(slot_token),
        "pos1": striped(pos[0]),
        "pos2": striped(pos[1]),
        "pos3": striped(pos[2]),
    }


def reference(uT, wu, w, b, gate, offs, pos1, pos2, pos3):
    idx = unstriped(offs)
    x = mxq(f64(wu), 0, "e4m3").T @ mxq(f64(uT), 0, "e4m3")
    xq = mxq(x[:, idx], 0, "e4m3")
    y = by_expert(mxq(f64(w), 1, "e4m3"), xq)
    y = y + np.repeat(f64(b), C, axis=1)
    return sum(f64(gate[r]) * y[:, unstriped(p)] for r, p in enumerate((pos1, pos2, pos3)))

@@ -1,0 +1,229 @@
+from contextlib import ExitStack
+
+import concourse.mybir as mybir
+
+M, K, T, E, C, N, TOP = 1024, 1024, 512, 6, 256, 256, 3
+S = E * C
+FLOPS = 2 * M * K * T + 2 * K * N * S
+BYTES = 4 * (M * T + M * K + E * K * N + N * E + TOP * T + N * T) + 2 * (S + TOP * T)
+
+F32 = mybir.dt.float32
+BF16 = mybir.dt.bfloat16
+I32 = mybir.dt.int32
+U32 = mybir.dt.uint32
+U16 = mybir.dt.uint16
+U8 = mybir.dt.uint8
+FP8X4 = mybir.dt.float8_e4m3fn_x4
+MULT = mybir.AluOpType.mult
+ADD = mybir.AluOpType.add
+IDENTITY = mybir.ActivationFunctionType.Identity
+
+P = 128
+PACK = 4
+PASS = P * PACK
+PASSES = 2
+HALF = T // 2
+PAIR = 2 * C
+PAIRS = E // 2
+WINDOW = 704
+PER_COL = 16
+
+
+def tile_moe_prv_lin_bias_kernel(tc, uT, wu, w, b, gate, offs, pos1, pos2, pos3, out):
+    nc = tc.nc
+    with ExitStack() as ctx:
+        lists = ctx.enter_context(tc.tile_pool(name="lists", bufs=1))
+        keep = ctx.enter_context(tc.tile_pool(name="keep", bufs=1))
+        stage = ctx.enter_context(tc.tile_pool(name="stage", bufs=4))
+        slots = ctx.enter_context(tc.tile_pool(name="slots", bufs=2))
+        xpsum = ctx.enter_context(tc.psum_pool(name="xpsum", bufs=4))
+        ypsum = ctx.enter_context(tc.psum_pool(name="ypsum", bufs=4))
+
+        def rows(g):
+            return slice(g * PASS, (g + 1) * PASS)
+
+        def load(name, src, width):
+            raw = keep.tile([P, PACK, width], F32, name=name)
+            nc.sync.dma_start(out=raw[:], in_=src.rearrange("(p j) c -> p j c", j=PACK))
+            return raw
+
+        def load_list(name, src, n):
+            held = lists.tile([P, n // PER_COL], U16, name=name)
+            nc.sync.dma_start(held[:], src)
+            return held
+
+        wu_raw, u_raw, w_raw = {}, {}, {}
+        for f in range(PASSES):
+            wu_raw[f, 0] = load("wu%d0" % f, wu[rows(f), rows(0)], PASS)
+        for h in range(2):
+            for f in range(PASSES):
+                u_raw[f, h] = load("u%d%d" % (f, h), uT[rows(f), h * HALF:(h + 1) * HALF], HALF)
+        offs_sb = load_list("offs_sb", offs, S)
+        wu_raw[0, 1] = load("wu01", wu[rows(0), rows(1)], PASS)
+        wu_raw[1, 1] = load("wu11", wu[rows(1), rows(1)], PASS)
+        for e in range(E):
+            w_raw[e] = keep.tile([P, PASSES, PACK, N], F32, name="w%d" % e, tag="w%d" % e)
+            nc.sync.dma_start(out=w_raw[e][:], in_=w[e].rearrange("(g p j) n -> p g j n", g=PASSES, j=PACK))
+        bias = keep.tile([P, 2, E], F32, name="bias")
+        nc.sync.dma_start(out=bias[:], in_=b.rearrange("(h p) e -> p h e", p=P))
+        gates = keep.tile([P, TOP, T], F32, name="gates")
+        nc.sync.dma_start(out=gates[:], in_=gate[:, 0:P, :].rearrange("r p t -> p r t"))
+        pos_sb = [load_list("pos%d" % r, src, T) for r, src in enumerate((pos1, pos2, pos3))]
+
+        def planes(name, width):
+            return (keep.tile([P, width], U32, name=name + "c", align_bytes=64),
+                    keep.tile([P, width], U8, name=name + "s", align_bytes=64))
+
+        u_q = [planes("uq%d" % f, T) for f in range(PASSES)]
+        wu_q = {(f, g, u): planes("wuq%d%d%d" % (f, g, u), 2 * P)
+                for f in range(PASSES) for g in range(PASSES) for u in range(2)}
+        w_q = {0: planes("wq0", E * PASSES * P)}
+        x_q = {(g, q): planes("xq%d%d" % (g, q), PAIR) for g in range(PASSES) for q in range(PAIRS)}
+        x_words = {(g, u): keep.tile([P, WINDOW], U32, name="x%d%d" % (g, u)) for g in range(PASSES) for u in range(2)}
+        for g in range(PASSES):
+            for u in range(2):
+                nc.gpsimd.memset(x_words[g, u][:, T:WINDOW], 0)
+        y = {1: keep.tile([P, S], F32, name="y1")}
+
+        def on_vector(dst, src):
+            nc.vector.tensor_copy(out=dst, in_=src)
+
+        def on_scalar(dst, src):
+            nc.scalar.copy(out=dst, in_=src)
+
+        def on_scalar_activation(dst, src):
+            nc.scalar.activation(out=dst, in_=src, func=IDENTITY)
+
+        def quantize(q, cols, grouped):
+            nc.vector.quantize_mx(out=q[0][:, cols].bitcast(FP8X4), scales=q[1][:, cols], in_=grouped)
+
+        def cast_wu(f, g, u, copy, pool=stage, tag="grouped"):
+            grouped = pool.tile([P, 2 * P * PACK], BF16, name="grouped", tag=tag, align_bytes=64)
+            copy(grouped[:].rearrange("p (e m j) -> p m j e", e=2, j=PACK),
+                 wu_raw[f, g][:].rearrange("p j (m t) -> p m j t", t=PACK)[:, :, :, 2 * u:2 * u + 2])
+            return grouped
+
+        def quantize_wu(f, g, u, grouped):
+            quantize(wu_q[f, g, u], slice(0, 2 * P), grouped[:])
+
+        def cast_u(raw, width):
+            grouped = stage.tile([P, width * PACK], BF16, name="grouped_u", tag="wide", align_bytes=64, bufs=3)
+            dst = grouped[:].rearrange("p (c i j) -> p c j i", i=4, j=PACK)
+            src = raw[:].rearrange("p j (c i) -> p c j i", i=4)
+            mid = width // 8
+            on_vector(dst[:, :mid], src[:, :mid])
+            on_scalar(dst[:, mid:], src[:, mid:])
+            return grouped
+
+        def shared_wu(f, g, scalar_copy):
+            grouped = [cast_wu(f, g, 0, on_vector), cast_wu(f, g, 1, scalar_copy)]
+            for u in range(2):
+                quantize_wu(f, g, u, grouped[u])
+
+        def project(g, u, h, copy):
+            bank = xpsum.tile([P, 2, HALF], F32, name="xbank")
+            tokens = slice(h * HALF, (h + 1) * HALF)
+            for e in range(2):
+                cols = slice(e * P, (e + 1) * P)
+                for f in range(PASSES):
+                    nc.tensor.matmul_mx(out=bank[:, e, :], lhsT=wu_q[f, g, u][0][:, cols].bitcast(FP8X4),
+                                        lhsT_scale=wu_q[f, g, u][1][:, cols],
+                                        rhs=u_q[f][0][:, tokens].bitcast(FP8X4), rhs_scale=u_q[f][1][:, tokens],
+                                        start=(f == 0), stop=(f == PASSES - 1))
+            pairs = x_words[g, u][:, tokens].bitcast(BF16).rearrange("p (c e) -> p c e", e=2)
+            copy(pairs, bank[:].rearrange("p e c -> p c e"))
+
+        def gather(g, q, pool, tag):
+            picked = pool.tile([P, 2, PAIR], U32, name="picked", tag=tag, align_bytes=64)
+            cols = slice(q * PAIR // PER_COL, (q + 1) * PAIR // PER_COL)
+            for u in range(2):
+                nc.vector.tensor_copy(out=picked[:, u, :], in_=x_words[g, u][:].indirect(offs_sb[:, cols]))
+            return picked
+
+        def weave(picked, engine, pool=slots, tag="woven"):
+            woven = pool.tile([P, 2 * PAIR], U32, name="woven", tag=tag, align_bytes=64)
+            view = I32 if engine == "vector" else U32
+            dst = woven[:].bitcast(view).rearrange("p (c i u) -> p c u i", i=2, u=2)
+            src = picked[:].bitcast(view).rearrange("p u (c i) -> p c u i", i=2)
+            (on_vector if engine == "vector" else on_scalar)(dst, src)
+            return woven
+
+        def quantize_x(g, q, woven):
+            quantize(x_q[g, q], slice(0, PAIR), woven[:].bitcast(BF16))
+
+        def cast_w(e, h, grouped):
+            on_scalar(grouped[:, e % 2, :].rearrange("p (g c i j) -> p g c j i", g=PASSES, i=4, j=PACK),
+                      w_raw[e][:, :, :, h * P:(h + 1) * P].rearrange("p g j (c i) -> p g c j i", i=4))
+
+        def quantize_w(q, h, grouped):
+            quantize(w_q[h], slice(q * PASS, (q + 1) * PASS), grouped[:].rearrange("p i c -> p (i c)"))
+
+        def experts(q, h):
+            banks = [ypsum.tile([P, C], F32, name="ybank") for i in range(2)]
+            for g in range(PASSES):
+                for i in range(2):
+                    e = 2 * q + i
+                    cols = slice(i * C, (i + 1) * C)
+                    wcols = slice((e * PASSES + g) * P, (e * PASSES + g + 1) * P)
+                    nc.tensor.matmul_mx(out=banks[i][:], lhsT=w_q[h][0][:, wcols].bitcast(FP8X4),
+                                        lhsT_scale=w_q[h][1][:, wcols],
+                                        rhs=x_q[g, q][0][:, cols].bitcast(FP8X4), rhs_scale=x_q[g, q][1][:, cols],
+                                        start=(g == 0), stop=(g == PASSES - 1))
+            for i in range(2):
+                e = 2 * q + i
+                nc.scalar.activation(out=y[h][:, e * C:(e + 1) * C], in_=banks[i][:], func=IDENTITY,
+                                     bias=bias[:, h, e:e + 1])
+
+        def combine(h):
+            terms = []
+            for r in range(TOP):
+                term = stage.tile([P, T], F32, name="term", tag="grouped", align_bytes=64)
+                nc.vector.tensor_tensor(term[:], y[h][:].indirect(pos_sb[r][:]), gates[:, r, :], MULT)
+                terms.append(term)
+            partial = stage.tile([P, T], F32, name="partial", tag="grouped", align_bytes=64)
+            nc.vector.tensor_tensor(partial[:], terms[0][:], terms[1][:], ADD)
+            total = keep.tile([P, T], F32, name="total%d" % h)
+            nc.vector.tensor_tensor(total[:], partial[:], terms[2][:], ADD)
+            nc.sync.dma_start(out=out[h * P:(h + 1) * P, :], in_=total[:])
+
+        shared_wu(0, 0, on_scalar_activation)
+        shared_wu(1, 0, on_scalar)
+        for h in range(2):
+            for f in range(PASSES):
+                quantize(u_q[f], slice(h * HALF, (h + 1) * HALF), cast_u(u_raw[f, h], HALF)[:])
+            project(0, 0, h, on_vector)
+            project(0, 1, h, on_scalar)
+        quantize_wu(0, 1, 0, cast_wu(0, 1, 0, on_scalar))
+        quantize_wu(0, 1, 1, cast_wu(0, 1, 1, on_scalar))
+        quantize_wu(1, 1, 0, cast_wu(1, 1, 0, on_scalar))
+        quantize_wu(1, 1, 1, cast_wu(1, 1, 1, on_scalar, keep, "after_wu"))
+        low = [keep.tile([P, 2, PASSES * PASS], BF16, name="w_low", tag="after_w%d" % q, align_bytes=64)
+               for q in range(PAIRS)]
+        quantize_x(0, 0, weave(gather(0, 0, slots, "picked"), "scalar"))
+        quantize_x(0, 1, weave(gather(0, 1, slots, "picked"), "scalar"))
+        for u in range(2):
+            for h in range(2):
+                project(1, u, h, on_scalar)
+        quantize_x(0, 2, weave(gather(0, 2, keep, "after_wu"), "scalar"))
+        for q in range(PAIRS):
+            for i in range(2):
+                cast_w(2 * q + i, 0, low[q])
+            quantize_w(q, 0, low[q])
+        high = [stage.tile([P, 2, PASSES * PASS], BF16, name="w_high", tag="wide", align_bytes=64, bufs=3)
+                for q in range(PAIRS)]
+        for e in range(E - 1):
+            cast_w(e, 1, high[e // 2])
+        y[0] = keep.tile([P, S], F32, name="y0", tag="w%d" % (E - 2))
+        quantize_x(1, 0, weave(gather(1, 0, slots, "picked"), "vector"))
+        quantize_x(1, 1, weave(gather(1, 1, keep, "after_w0"), "vector"))
+        quantize_x(1, 2, weave(gather(1, 2, keep, "after_w1"), "vector", keep, "after_w2"))
+        for q in range(PAIRS):
+            experts(q, 0)
+        cast_w(E - 1, 1, high[-1])
+        w_q[1] = (keep.tile([P, E * PASSES * P], U32, name="wq1c", tag="after_w2", align_bytes=64),
+                  keep.tile([P, E * PASSES * P], U8, name="wq1s", align_bytes=64))
+        for q in range(PAIRS):
+            quantize_w(q, 1, high[q])
+            experts(q, 1)
+        combine(0)
+        combine(1)

@@ -1,6 +1,7 @@
 from contextlib import ExitStack
 
 import concourse.mybir as mybir
+from concourse.masks import make_identity
 
 M, K, T, E, C, N, TOP = 1024, 1024, 512, 6, 256, 256, 3
 S = E * C
@@ -16,6 +17,7 @@ U8 = mybir.dt.uint8
 FP8X4 = mybir.dt.float8_e4m3fn_x4
 MULT = mybir.AluOpType.mult
 ADD = mybir.AluOpType.add
+COPY = mybir.ActivationFunctionType.Copy
 IDENTITY = mybir.ActivationFunctionType.Identity
 
 P = 128
@@ -36,14 +38,13 @@ def tile_moe_prv_lin_bias_kernel(tc, uT, wu, w, b, gate, offs, pos1, pos2, pos3,
         keep = ctx.enter_context(tc.tile_pool(name="keep", bufs=1))
         stage = ctx.enter_context(tc.tile_pool(name="stage", bufs=4))
         slots = ctx.enter_context(tc.tile_pool(name="slots", bufs=2))
-        xpsum = ctx.enter_context(tc.psum_pool(name="xpsum", bufs=4))
-        ypsum = ctx.enter_context(tc.psum_pool(name="ypsum", bufs=4))
+        psum = ctx.enter_context(tc.psum_pool(name="psum", bufs=6))
 
         def rows(g):
             return slice(g * PASS, (g + 1) * PASS)
 
         def load(name, src, width):
-            raw = keep.tile([P, PACK, width], F32, name=name)
+            raw = keep.tile([P, PACK, width], F32, name=name, tag=name, align_bytes=64)
             nc.sync.dma_start(out=raw[:], in_=src.rearrange("(p j) c -> p j c", j=PACK))
             return raw
 
@@ -62,13 +63,21 @@ def tile_moe_prv_lin_bias_kernel(tc, uT, wu, w, b, gate, offs, pos1, pos2, pos3,
         wu_raw[0, 1] = load("wu01", wu[rows(0), rows(1)], PASS)
         wu_raw[1, 1] = load("wu11", wu[rows(1), rows(1)], PASS)
         for e in range(E):
-            w_raw[e] = keep.tile([P, PASSES, PACK, N], F32, name="w%d" % e, tag="w%d" % e)
+            w_raw[e] = keep.tile([P, PASSES, PACK, N], F32, name="w%d" % e, tag="w%d" % e, align_bytes=64)
             nc.sync.dma_start(out=w_raw[e][:], in_=w[e].rearrange("(g p j) n -> p g j n", g=PASSES, j=PACK))
-        bias = keep.tile([P, 2, E], F32, name="bias")
+        bias = keep.tile([P, 2, E], F32, name="bias", tag="bias", align_bytes=64)
         nc.sync.dma_start(out=bias[:], in_=b.rearrange("(h p) e -> p h e", p=P))
-        gates = keep.tile([P, TOP, T], F32, name="gates")
-        nc.sync.dma_start(out=gates[:], in_=gate[:, 0:P, :].rearrange("r p t -> p r t"))
+        gate_rows = keep.tile([P, TOP, T], F32, name="gate_rows")
+        nc.sync.dma_start(out=gate_rows[:], in_=gate[:, 0:P, :].rearrange("r p t -> p r t"))
         pos_sb = [load_list("pos%d" % r, src, T) for r, src in enumerate((pos1, pos2, pos3))]
+        gate_cols = []
+        for r in range(TOP):
+            column = keep.tile([P, T // P], F32, name="gate_col%d" % r)
+            with nc.allow_non_contiguous_dma(reason="one gate value for each partition"):
+                nc.sync.dma_start(out=column[:], in_=gate[r, 0, :].rearrange("(c p) -> p c", p=P))
+            gate_cols.append(column)
+        identity = keep.tile([P, P], F32, name="identity")
+        make_identity(nc, identity[:])
 
         def planes(name, width):
             return (keep.tile([P, width], U32, name=name + "c", align_bytes=64),
@@ -77,13 +86,13 @@ def tile_moe_prv_lin_bias_kernel(tc, uT, wu, w, b, gate, offs, pos1, pos2, pos3,
         u_q = [planes("uq%d" % f, T) for f in range(PASSES)]
         wu_q = {(f, g, u): planes("wuq%d%d%d" % (f, g, u), 2 * P)
                 for f in range(PASSES) for g in range(PASSES) for u in range(2)}
-        w_q = {0: planes("wq0", E * PASSES * P)}
+        w_q = [planes("wq%d" % h, E * PASSES * P) for h in range(2)]
         x_q = {(g, q): planes("xq%d%d" % (g, q), PAIR) for g in range(PASSES) for q in range(PAIRS)}
         x_words = {(g, u): keep.tile([P, WINDOW], U32, name="x%d%d" % (g, u)) for g in range(PASSES) for u in range(2)}
         for g in range(PASSES):
             for u in range(2):
                 nc.gpsimd.memset(x_words[g, u][:, T:WINDOW], 0)
-        y = {1: keep.tile([P, S], F32, name="y1")}
+        y = {}
 
         def on_vector(dst, src):
             nc.vector.tensor_copy(out=dst, in_=src)
@@ -97,8 +106,8 @@ def tile_moe_prv_lin_bias_kernel(tc, uT, wu, w, b, gate, offs, pos1, pos2, pos3,
         def quantize(q, cols, grouped):
             nc.vector.quantize_mx(out=q[0][:, cols].bitcast(FP8X4), scales=q[1][:, cols], in_=grouped)
 
-        def cast_wu(f, g, u, copy, pool=stage, tag="grouped"):
-            grouped = pool.tile([P, 2 * P * PACK], BF16, name="grouped", tag=tag, align_bytes=64)
+        def cast_wu(f, g, u, copy):
+            grouped = stage.tile([P, 2 * P * PACK], BF16, name="grouped", align_bytes=64)
             copy(grouped[:].rearrange("p (e m j) -> p m j e", e=2, j=PACK),
                  wu_raw[f, g][:].rearrange("p j (m t) -> p m j t", t=PACK)[:, :, :, 2 * u:2 * u + 2])
             return grouped
@@ -110,7 +119,7 @@ def tile_moe_prv_lin_bias_kernel(tc, uT, wu, w, b, gate, offs, pos1, pos2, pos3,
             grouped = stage.tile([P, width * PACK], BF16, name="grouped_u", tag="wide", align_bytes=64, bufs=3)
             dst = grouped[:].rearrange("p (c i j) -> p c j i", i=4, j=PACK)
             src = raw[:].rearrange("p j (c i) -> p c j i", i=4)
-            mid = width // 8
+            mid = width // 4 * 5 // 8
             on_vector(dst[:, :mid], src[:, :mid])
             on_scalar(dst[:, mid:], src[:, mid:])
             return grouped
@@ -121,7 +130,7 @@ def tile_moe_prv_lin_bias_kernel(tc, uT, wu, w, b, gate, offs, pos1, pos2, pos3,
                 quantize_wu(f, g, u, grouped[u])
 
         def project(g, u, h, copy):
-            bank = xpsum.tile([P, 2, HALF], F32, name="xbank")
+            bank = psum.tile([P, 2, HALF], F32, name="bank")
             tokens = slice(h * HALF, (h + 1) * HALF)
             for e in range(2):
                 cols = slice(e * P, (e + 1) * P)
@@ -133,23 +142,29 @@ def tile_moe_prv_lin_bias_kernel(tc, uT, wu, w, b, gate, offs, pos1, pos2, pos3,
             pairs = x_words[g, u][:, tokens].bitcast(BF16).rearrange("p (c e) -> p c e", e=2)
             copy(pairs, bank[:].rearrange("p e c -> p c e"))
 
-        def gather(g, q, pool, tag):
-            picked = pool.tile([P, 2, PAIR], U32, name="picked", tag=tag, align_bytes=64)
+        def unit(tag):
+            return slots.tile([P, 2 * PAIR], U32, name=tag, tag=tag, align_bytes=64)[:]
+
+        def units_after(tag, count):
+            joint = keep.tile([P, count * 2 * PAIR], U32, name="units", tag=tag, align_bytes=64)
+            return [joint[:, n * 2 * PAIR:(n + 1) * 2 * PAIR] for n in range(count)]
+
+        def gather(g, q, picked):
             cols = slice(q * PAIR // PER_COL, (q + 1) * PAIR // PER_COL)
             for u in range(2):
-                nc.vector.tensor_copy(out=picked[:, u, :], in_=x_words[g, u][:].indirect(offs_sb[:, cols]))
+                nc.vector.tensor_copy(out=picked[:, u * PAIR:(u + 1) * PAIR],
+                                      in_=x_words[g, u][:].indirect(offs_sb[:, cols]))
             return picked
 
-        def weave(picked, engine, pool=slots, tag="woven"):
-            woven = pool.tile([P, 2 * PAIR], U32, name="woven", tag=tag, align_bytes=64)
+        def weave(picked, woven, engine="vector"):
             view = I32 if engine == "vector" else U32
-            dst = woven[:].bitcast(view).rearrange("p (c i u) -> p c u i", i=2, u=2)
-            src = picked[:].bitcast(view).rearrange("p u (c i) -> p c u i", i=2)
+            dst = woven.bitcast(view).rearrange("p (c i u) -> p c u i", i=2, u=2)
+            src = picked.bitcast(view).rearrange("p (u c i) -> p c u i", u=2, i=2)
             (on_vector if engine == "vector" else on_scalar)(dst, src)
             return woven
 
         def quantize_x(g, q, woven):
-            quantize(x_q[g, q], slice(0, PAIR), woven[:].bitcast(BF16))
+            quantize(x_q[g, q], slice(0, PAIR), woven.bitcast(BF16))
 
         def cast_w(e, h, grouped):
             on_scalar(grouped[:, e % 2, :].rearrange("p (g c i j) -> p g c j i", g=PASSES, i=4, j=PACK),
@@ -159,7 +174,7 @@ def tile_moe_prv_lin_bias_kernel(tc, uT, wu, w, b, gate, offs, pos1, pos2, pos3,
             quantize(w_q[h], slice(q * PASS, (q + 1) * PASS), grouped[:].rearrange("p i c -> p (i c)"))
 
         def experts(q, h):
-            banks = [ypsum.tile([P, C], F32, name="ybank") for i in range(2)]
+            banks = [psum.tile([P, C], F32, name="bank") for i in range(2)]
             for g in range(PASSES):
                 for i in range(2):
                     e = 2 * q + i
@@ -174,56 +189,87 @@ def tile_moe_prv_lin_bias_kernel(tc, uT, wu, w, b, gate, offs, pos1, pos2, pos3,
                 nc.scalar.activation(out=y[h][:, e * C:(e + 1) * C], in_=banks[i][:], func=IDENTITY,
                                      bias=bias[:, h, e:e + 1])
 
-        def combine(h):
-            terms = []
+        def combine_turned(h):
+            scaled = keep.tile([P, TOP, T], F32, name="scaled", tag="wu00", align_bytes=64)
             for r in range(TOP):
-                term = stage.tile([P, T], F32, name="term", tag="grouped", align_bytes=64)
-                nc.vector.tensor_tensor(term[:], y[h][:].indirect(pos_sb[r][:]), gates[:, r, :], MULT)
-                terms.append(term)
-            partial = stage.tile([P, T], F32, name="partial", tag="grouped", align_bytes=64)
-            nc.vector.tensor_tensor(partial[:], terms[0][:], terms[1][:], ADD)
+                fetched = stage.tile([P, T], F32, name="fetched", tag="grouped", align_bytes=64)
+                nc.vector.tensor_copy(out=fetched[:], in_=y[h][:].indirect(pos_sb[r][:]))
+                bank = psum.tile([P, T], F32, name="bank")
+                for c in range(T // P):
+                    cols = slice(c * P, (c + 1) * P)
+                    nc.tensor.transpose(bank[:, cols], fetched[:, cols], identity[:])
+                for c in range(T // P):
+                    cols = slice(c * P, (c + 1) * P)
+                    nc.scalar.activation(out=scaled[:, r, cols], in_=bank[:, cols], func=COPY,
+                                         scale=gate_cols[r][:, c:c + 1])
+            summed = psum.tile([P, T], F32, name="bank")
+            for c in range(T // P):
+                cols = slice(c * P, (c + 1) * P)
+                for r in range(TOP):
+                    nc.tensor.matmul(summed[:, cols], scaled[:, r, cols], identity[:], is_transpose=True,
+                                     start=(r == 0), stop=(r == TOP - 1))
             total = keep.tile([P, T], F32, name="total%d" % h)
-            nc.vector.tensor_tensor(total[:], partial[:], terms[2][:], ADD)
-            nc.sync.dma_start(out=out[h * P:(h + 1) * P, :], in_=total[:])
+            on_scalar(total[:], summed[:])
+            nc.scalar.dma_start(out=out[h * P:(h + 1) * P, :], in_=total[:])
+
+        def combine_fused(h):
+            terms = keep.tile([P, TOP * T], F32, name="terms", tag="wu10", align_bytes=64)
+            for r in range(TOP):
+                nc.vector.tensor_tensor(terms[:, r * T:(r + 1) * T], y[h][:].indirect(pos_sb[r][:]),
+                                        gate_rows[:, r, :], MULT)
+            partial = keep.tile([P, T], F32, name="partial")
+            total = keep.tile([P, T], F32, name="total%d" % h)
+            halves = [slice(n * HALF, (n + 1) * HALF) for n in range(2)]
+            for n in range(2):
+                nc.vector.tensor_tensor(partial[:, halves[n]], terms[:, n * HALF:(n + 1) * HALF],
+                                        terms[:, T + n * HALF:T + (n + 1) * HALF], ADD)
+            for n in range(2):
+                nc.vector.tensor_tensor(total[:, halves[n]], partial[:, halves[n]],
+                                        terms[:, 2 * T + n * HALF:2 * T + (n + 1) * HALF], ADD)
+                nc.sync.dma_start(out=out[h * P:(h + 1) * P, halves[n]], in_=total[:, halves[n]])
 
         shared_wu(0, 0, on_scalar_activation)
         shared_wu(1, 0, on_scalar)
         for h in range(2):
             for f in range(PASSES):
                 quantize(u_q[f], slice(h * HALF, (h + 1) * HALF), cast_u(u_raw[f, h], HALF)[:])
-            project(0, 0, h, on_vector)
+            project(0, 0, h, on_vector if h == 1 else on_scalar)
             project(0, 1, h, on_scalar)
-        quantize_wu(0, 1, 0, cast_wu(0, 1, 0, on_scalar))
-        quantize_wu(0, 1, 1, cast_wu(0, 1, 1, on_scalar))
-        quantize_wu(1, 1, 0, cast_wu(1, 1, 0, on_scalar))
-        quantize_wu(1, 1, 1, cast_wu(1, 1, 1, on_scalar, keep, "after_wu"))
-        low = [keep.tile([P, 2, PASSES * PASS], BF16, name="w_low", tag="after_w%d" % q, align_bytes=64)
-               for q in range(PAIRS)]
-        quantize_x(0, 0, weave(gather(0, 0, slots, "picked"), "scalar"))
-        quantize_x(0, 1, weave(gather(0, 1, slots, "picked"), "scalar"))
+        for f in range(PASSES):
+            for u in range(2):
+                quantize_wu(f, 1, u, cast_wu(f, 1, u, on_scalar))
+        low = [keep.tile([P, 2, PASSES * PASS], BF16, name="low%d" % q, align_bytes=64) for q in range(PAIRS)]
+        high = [stage.tile([P, 2, PASSES * PASS], BF16, name="w_high", tag="wide", align_bytes=64, bufs=3)
+                for q in range(PAIRS)]
+        picked = [gather(0, q, unit("picked")) for q in range(2)]
+        after_wu = units_after("wu11", 3)
+        woven = [weave(picked[q], after_wu[q], ("scalar", "vector")[q]) for q in range(2)]
+        for e, h in ((0, 0), (1, 0)):
+            cast_w(e, h, (low, high)[h][e // 2])
         for u in range(2):
             for h in range(2):
                 project(1, u, h, on_scalar)
-        quantize_x(0, 2, weave(gather(0, 2, keep, "after_wu"), "scalar"))
-        for q in range(PAIRS):
-            for i in range(2):
-                cast_w(2 * q + i, 0, low[q])
-            quantize_w(q, 0, low[q])
-        high = [stage.tile([P, 2, PASSES * PASS], BF16, name="w_high", tag="wide", align_bytes=64, bufs=3)
-                for q in range(PAIRS)]
-        for e in range(E - 1):
-            cast_w(e, 1, high[e // 2])
-        y[0] = keep.tile([P, S], F32, name="y0", tag="w%d" % (E - 2))
-        quantize_x(1, 0, weave(gather(1, 0, slots, "picked"), "vector"))
-        quantize_x(1, 1, weave(gather(1, 1, keep, "after_w0"), "vector"))
-        quantize_x(1, 2, weave(gather(1, 2, keep, "after_w1"), "vector", keep, "after_w2"))
+        quantize_x(0, 0, woven[0])
+        gather(0, 2, after_wu[2])
+        quantize_x(0, 1, woven[1])
+        quantize_x(0, 2, weave(after_wu[2], unit("woven"), "vector"))
+        quantize_w(0, 0, low[0])
+        picked = [gather(1, q, unit("picked")) for q in range(2)]
+        quantize_x(1, 0, weave(picked[0], unit("woven"), "vector"))
+        for e, h in ((2, 0), (3, 0), (3, 1), (4, 0), (5, 0), (1, 1), (0, 1), (5, 1), (2, 1), (4, 1)):
+            cast_w(e, h, (low, high)[h][e // 2])
+        quantize_w(1, 0, low[1])
+        after_w3 = units_after("w3", 2)
+        quantize_x(1, 1, weave(picked[1], after_w3[0]))
+        gather(1, 2, after_w3[1])
+        quantize_w(2, 0, low[2])
+        quantize_x(1, 2, weave(after_w3[1], units_after("w0", 1)[0]))
+        y[0] = keep.tile([P, S], F32, name="y0", tag="w2", align_bytes=64)
+        y[1] = keep.tile([P, S], F32, name="y1", tag="w4", align_bytes=64)
         for q in range(PAIRS):
             experts(q, 0)
-        cast_w(E - 1, 1, high[-1])
-        w_q[1] = (keep.tile([P, E * PASSES * P], U32, name="wq1c", tag="after_w2", align_bytes=64),
-                  keep.tile([P, E * PASSES * P], U8, name="wq1s", align_bytes=64))
         for q in range(PAIRS):
             quantize_w(q, 1, high[q])
             experts(q, 1)
-        combine(0)
-        combine(1)
+        combine_turned(0)
+        combine_fused(1)

@@ -27,7 +27,11 @@ PASSES = 2
 HALF = T // 2
 PAIR = 2 * C
 PAIRS = E // 2
+QUARTER = T // 4
+U_PIECES = ((0, 0, HALF), (1, 0, HALF), (0, HALF, T), (1, HALF, T - QUARTER), (1, T - QUARTER, T))
 WINDOW = 704
+UNIT_BYTES = 4096
+REGIONS = {"wu11": 0, "w3": 8192, "w0": 16384}
 PER_COL = 16
 
 
@@ -36,15 +40,24 @@ def tile_moe_prv_lin_bias_kernel(tc, uT, wu, w, b, gate, offs, pos1, pos2, pos3,
     with ExitStack() as ctx:
         lists = ctx.enter_context(tc.tile_pool(name="lists", bufs=1))
         keep = ctx.enter_context(tc.tile_pool(name="keep", bufs=1))
+        placed = ctx.enter_context(tc.tile_pool(name="placed", bufs=1))
         stage = ctx.enter_context(tc.tile_pool(name="stage", bufs=4))
-        slots = ctx.enter_context(tc.tile_pool(name="slots", bufs=2))
+        slots = ctx.enter_context(tc.tile_pool(name="slots", bufs=3))
         psum = ctx.enter_context(tc.psum_pool(name="psum", bufs=6))
 
         def rows(g):
             return slice(g * PASS, (g + 1) * PASS)
 
+        def raw_tile(name, shape):
+            if name in REGIONS:
+                return placed.tile(shape, F32, name=name, offset=REGIONS[name], align_bytes=64)
+            return keep.tile(shape, F32, name=name, tag=name, align_bytes=64)
+
+        def follower(region, at, name, width):
+            return placed.tile([P, width], U32, name=name, offset=REGIONS[region] + at, align_bytes=64)
+
         def load(name, src, width):
-            raw = keep.tile([P, PACK, width], F32, name=name, tag=name, align_bytes=64)
+            raw = raw_tile(name, [P, PACK, width])
             nc.sync.dma_start(out=raw[:], in_=src.rearrange("(p j) c -> p j c", j=PACK))
             return raw
 
@@ -56,14 +69,13 @@ def tile_moe_prv_lin_bias_kernel(tc, uT, wu, w, b, gate, offs, pos1, pos2, pos3,
         wu_raw, u_raw, w_raw = {}, {}, {}
         for f in range(PASSES):
             wu_raw[f, 0] = load("wu%d0" % f, wu[rows(f), rows(0)], PASS)
-        for h in range(2):
-            for f in range(PASSES):
-                u_raw[f, h] = load("u%d%d" % (f, h), uT[rows(f), h * HALF:(h + 1) * HALF], HALF)
+        for n, (f, lo, hi) in enumerate(U_PIECES):
+            u_raw[n] = load("u%d" % n, uT[rows(f), lo:hi], hi - lo)
         offs_sb = load_list("offs_sb", offs, S)
         wu_raw[0, 1] = load("wu01", wu[rows(0), rows(1)], PASS)
         wu_raw[1, 1] = load("wu11", wu[rows(1), rows(1)], PASS)
         for e in range(E):
-            w_raw[e] = keep.tile([P, PASSES, PACK, N], F32, name="w%d" % e, tag="w%d" % e, align_bytes=64)
+            w_raw[e] = raw_tile("w%d" % e, [P, PASSES, PACK, N])
             nc.sync.dma_start(out=w_raw[e][:], in_=w[e].rearrange("(g p j) n -> p g j n", g=PASSES, j=PACK))
         bias = keep.tile([P, 2, E], F32, name="bias", tag="bias", align_bytes=64)
         nc.sync.dma_start(out=bias[:], in_=b.rearrange("(h p) e -> p h e", p=P))
@@ -84,14 +96,12 @@ def tile_moe_prv_lin_bias_kernel(tc, uT, wu, w, b, gate, offs, pos1, pos2, pos3,
                     keep.tile([P, width], U8, name=name + "s", align_bytes=64))
 
         u_q = [planes("uq%d" % f, T) for f in range(PASSES)]
-        wu_q = {(f, g, u): planes("wuq%d%d%d" % (f, g, u), 2 * P)
-                for f in range(PASSES) for g in range(PASSES) for u in range(2)}
+        wu_q = {(f, g): planes("wuq%d%d" % (f, g), PASS) for f in range(PASSES) for g in range(PASSES)}
         w_q = [planes("wq%d" % h, E * PASSES * P) for h in range(2)]
         x_q = {(g, q): planes("xq%d%d" % (g, q), PAIR) for g in range(PASSES) for q in range(PAIRS)}
-        x_words = {(g, u): keep.tile([P, WINDOW], U32, name="x%d%d" % (g, u)) for g in range(PASSES) for u in range(2)}
-        for g in range(PASSES):
-            for u in range(2):
-                nc.gpsimd.memset(x_words[g, u][:, T:WINDOW], 0)
+        x_words = {(0, u): keep.tile([P, WINDOW], U32, name="x0%d" % u) for u in range(2)}
+        for u in range(2):
+            nc.gpsimd.memset(x_words[0, u][:, T:WINDOW], 0)
         y = {}
 
         def on_vector(dst, src):
@@ -106,37 +116,39 @@ def tile_moe_prv_lin_bias_kernel(tc, uT, wu, w, b, gate, offs, pos1, pos2, pos3,
         def quantize(q, cols, grouped):
             nc.vector.quantize_mx(out=q[0][:, cols].bitcast(FP8X4), scales=q[1][:, cols], in_=grouped)
 
-        def cast_wu(f, g, u, copy):
-            grouped = stage.tile([P, 2 * P * PACK], BF16, name="grouped", align_bytes=64)
-            copy(grouped[:].rearrange("p (e m j) -> p m j e", e=2, j=PACK),
+        def cast_wu(f, g, u, copy, grouped):
+            copy(grouped.rearrange("p (e m j) -> p m j e", e=2, j=PACK),
                  wu_raw[f, g][:].rearrange("p j (m t) -> p m j t", t=PACK)[:, :, :, 2 * u:2 * u + 2])
             return grouped
 
-        def quantize_wu(f, g, u, grouped):
-            quantize(wu_q[f, g, u], slice(0, 2 * P), grouped[:])
+        def staging():
+            return stage.tile([P, 2 * P * PACK], BF16, name="grouped", tag="grouped", align_bytes=64)[:]
 
-        def cast_u(raw, width):
-            grouped = stage.tile([P, width * PACK], BF16, name="grouped_u", tag="wide", align_bytes=64, bufs=3)
-            dst = grouped[:].rearrange("p (c i j) -> p c j i", i=4, j=PACK)
+        def quantize_wu(f, g, u, grouped):
+            quantize(wu_q[f, g], slice(u * 2 * P, (u + 1) * 2 * P), grouped)
+
+        def cast_u(raw, grouped, shared):
+            dst = grouped.rearrange("p (c i j) -> p c j i", i=4, j=PACK)
             src = raw[:].rearrange("p j (c i) -> p c j i", i=4)
-            mid = width // 4 * 5 // 8
+            mid = src.shape[1] * 5 // 8 if shared else src.shape[1]
             on_vector(dst[:, :mid], src[:, :mid])
-            on_scalar(dst[:, mid:], src[:, mid:])
+            if shared:
+                on_scalar(dst[:, mid:], src[:, mid:])
             return grouped
 
         def shared_wu(f, g, scalar_copy):
-            grouped = [cast_wu(f, g, 0, on_vector), cast_wu(f, g, 1, scalar_copy)]
+            grouped = [cast_wu(f, g, 0, on_vector, staging()), cast_wu(f, g, 1, scalar_copy, staging())]
             for u in range(2):
                 quantize_wu(f, g, u, grouped[u])
 
-        def project(g, u, h, copy):
-            bank = psum.tile([P, 2, HALF], F32, name="bank")
-            tokens = slice(h * HALF, (h + 1) * HALF)
+        def project(g, u, lo, hi, copy, tag="bank", bufs=6):
+            bank = psum.tile([P, 2, hi - lo], F32, name="bank", tag=tag, bufs=bufs)
+            tokens = slice(lo, hi)
             for e in range(2):
-                cols = slice(e * P, (e + 1) * P)
+                cols = slice((2 * u + e) * P, (2 * u + e + 1) * P)
                 for f in range(PASSES):
-                    nc.tensor.matmul_mx(out=bank[:, e, :], lhsT=wu_q[f, g, u][0][:, cols].bitcast(FP8X4),
-                                        lhsT_scale=wu_q[f, g, u][1][:, cols],
+                    nc.tensor.matmul_mx(out=bank[:, e, :], lhsT=wu_q[f, g][0][:, cols].bitcast(FP8X4),
+                                        lhsT_scale=wu_q[f, g][1][:, cols],
                                         rhs=u_q[f][0][:, tokens].bitcast(FP8X4), rhs_scale=u_q[f][1][:, tokens],
                                         start=(f == 0), stop=(f == PASSES - 1))
             pairs = x_words[g, u][:, tokens].bitcast(BF16).rearrange("p (c e) -> p c e", e=2)
@@ -144,10 +156,6 @@ def tile_moe_prv_lin_bias_kernel(tc, uT, wu, w, b, gate, offs, pos1, pos2, pos3,
 
         def unit(tag):
             return slots.tile([P, 2 * PAIR], U32, name=tag, tag=tag, align_bytes=64)[:]
-
-        def units_after(tag, count):
-            joint = keep.tile([P, count * 2 * PAIR], U32, name="units", tag=tag, align_bytes=64)
-            return [joint[:, n * 2 * PAIR:(n + 1) * 2 * PAIR] for n in range(count)]
 
         def gather(g, q, picked):
             cols = slice(q * PAIR // PER_COL, (q + 1) * PAIR // PER_COL)
@@ -167,11 +175,11 @@ def tile_moe_prv_lin_bias_kernel(tc, uT, wu, w, b, gate, offs, pos1, pos2, pos3,
             quantize(x_q[g, q], slice(0, PAIR), woven.bitcast(BF16))
 
         def cast_w(e, h, grouped):
-            on_scalar(grouped[:, e % 2, :].rearrange("p (g c i j) -> p g c j i", g=PASSES, i=4, j=PACK),
+            on_scalar(grouped[:, (e % 2) * PASSES * PASS:(e % 2 + 1) * PASSES * PASS].rearrange("p (g c i j) -> p g c j i", g=PASSES, i=4, j=PACK),
                       w_raw[e][:, :, :, h * P:(h + 1) * P].rearrange("p g j (c i) -> p g c j i", i=4))
 
         def quantize_w(q, h, grouped):
-            quantize(w_q[h], slice(q * PASS, (q + 1) * PASS), grouped[:].rearrange("p i c -> p (i c)"))
+            quantize(w_q[h], slice(q * PASS, (q + 1) * PASS), grouped)
 
         def experts(q, h):
             banks = [psum.tile([P, C], F32, name="bank") for i in range(2)]
@@ -230,40 +238,43 @@ def tile_moe_prv_lin_bias_kernel(tc, uT, wu, w, b, gate, offs, pos1, pos2, pos3,
 
         shared_wu(0, 0, on_scalar_activation)
         shared_wu(1, 0, on_scalar)
-        for h in range(2):
-            for f in range(PASSES):
-                quantize(u_q[f], slice(h * HALF, (h + 1) * HALF), cast_u(u_raw[f, h], HALF)[:])
-            project(0, 0, h, on_vector if h == 1 else on_scalar)
-            project(0, 1, h, on_scalar)
+        for n, (f, lo, hi) in enumerate(U_PIECES):
+            grouped = stage.tile([P, (hi - lo) * PACK], BF16, name="grouped_u", tag="wide", align_bytes=64, bufs=3)
+            quantize(u_q[f], slice(lo, hi), cast_u(u_raw[n], grouped[:], hi - lo == HALF))
+        project(0, 0, 0, HALF, on_scalar)
+        project(0, 0, HALF, T - QUARTER, on_scalar)
+        project(0, 0, T - QUARTER, T, on_vector, "first", 1)
+        project(0, 1, HALF, T, on_scalar)
+        project(0, 1, 0, HALF, on_scalar, "first", 1)
         for f in range(PASSES):
             for u in range(2):
-                quantize_wu(f, 1, u, cast_wu(f, 1, u, on_scalar))
-        low = [keep.tile([P, 2, PASSES * PASS], BF16, name="low%d" % q, align_bytes=64) for q in range(PAIRS)]
-        high = [stage.tile([P, 2, PASSES * PASS], BF16, name="w_high", tag="wide", align_bytes=64, bufs=3)
+                quantize_wu(f, 1, u, cast_wu(f, 1, u, on_scalar, staging()))
+        low = [keep.tile([P, 2 * PASSES * PASS], BF16, name="low%d" % q, align_bytes=64)[:] for q in range(PAIRS)]
+        high = [stage.tile([P, 2 * PASSES * PASS], BF16, name="high", tag="wide", align_bytes=64, bufs=3)[:]
                 for q in range(PAIRS)]
-        picked = [gather(0, q, unit("picked")) for q in range(2)]
-        after_wu = units_after("wu11", 3)
-        woven = [weave(picked[q], after_wu[q], ("scalar", "vector")[q]) for q in range(2)]
-        for e, h in ((0, 0), (1, 0)):
+        picked = [gather(0, q, unit("picked")) for q in range(PAIRS)]
+        woven = [weave(picked[q], follower("wu11", q * UNIT_BYTES, "woven0%d" % q, 2 * PAIR)[:], ("vector", "vector")[q])
+                 for q in range(2)]
+        for e, h in ((0, 0), (0, 1), (1, 0)):
             cast_w(e, h, (low, high)[h][e // 2])
         for u in range(2):
+            x_words[1, u] = follower("w0", u * WINDOW * 4, "x1%d" % u, WINDOW)
+            nc.gpsimd.memset(x_words[1, u][:, T:WINDOW], 0)
             for h in range(2):
-                project(1, u, h, on_scalar)
+                project(1, u, h * HALF, (h + 1) * HALF, on_scalar)
         quantize_x(0, 0, woven[0])
-        gather(0, 2, after_wu[2])
         quantize_x(0, 1, woven[1])
-        quantize_x(0, 2, weave(after_wu[2], unit("woven"), "vector"))
+        quantize_x(0, 2, weave(picked[2], follower("w0", 2 * WINDOW * 4, "woven02", 2 * PAIR)[:], "scalar"))
         quantize_w(0, 0, low[0])
         picked = [gather(1, q, unit("picked")) for q in range(2)]
         quantize_x(1, 0, weave(picked[0], unit("woven"), "vector"))
-        for e, h in ((2, 0), (3, 0), (3, 1), (4, 0), (5, 0), (1, 1), (0, 1), (5, 1), (2, 1), (4, 1)):
+        for e, h in ((2, 0), (3, 0), (3, 1), (4, 0), (5, 0), (1, 1), (5, 1), (2, 1), (4, 1)):
             cast_w(e, h, (low, high)[h][e // 2])
         quantize_w(1, 0, low[1])
-        after_w3 = units_after("w3", 2)
-        quantize_x(1, 1, weave(picked[1], after_w3[0]))
-        gather(1, 2, after_w3[1])
+        quantize_x(1, 1, weave(picked[1], follower("w3", 0, "woven11", 2 * PAIR)[:]))
+        last = gather(1, 2, follower("w3", UNIT_BYTES, "picked12", 2 * PAIR)[:])
         quantize_w(2, 0, low[2])
-        quantize_x(1, 2, weave(after_w3[1], units_after("w0", 1)[0]))
+        quantize_x(1, 2, weave(last, keep.tile([P, 2 * PAIR], U32, name="woven12", tag="w1", align_bytes=64)[:]))
         y[0] = keep.tile([P, S], F32, name="y0", tag="w2", align_bytes=64)
         y[1] = keep.tile([P, S], F32, name="y1", tag="w4", align_bytes=64)
         for q in range(PAIRS):

@@ -28,10 +28,9 @@ HALF = T // 2
 PAIR = 2 * C
 PAIRS = E // 2
 QUARTER = T // 4
-U_PIECES = ((0, 0, HALF), (1, 0, HALF), (0, HALF, T), (1, HALF, T - QUARTER), (1, T - QUARTER, T))
 WINDOW = 704
 UNIT_BYTES = 4096
-REGIONS = {"wu11": 0, "w3": 8192, "w0": 16384}
+REGIONS = {"wu11": 2048, "w3": 12288, "w0": 20480, "wu01": 30720, "w5": 40960}
 PER_COL = 16
 
 
@@ -42,7 +41,7 @@ def tile_moe_prv_lin_bias_kernel(tc, uT, wu, w, b, gate, offs, pos1, pos2, pos3,
         keep = ctx.enter_context(tc.tile_pool(name="keep", bufs=1))
         placed = ctx.enter_context(tc.tile_pool(name="placed", bufs=1))
         stage = ctx.enter_context(tc.tile_pool(name="stage", bufs=4))
-        slots = ctx.enter_context(tc.tile_pool(name="slots", bufs=3))
+        slots = ctx.enter_context(tc.tile_pool(name="slots", bufs=2))
         psum = ctx.enter_context(tc.psum_pool(name="psum", bufs=6))
 
         def rows(g):
@@ -53,8 +52,8 @@ def tile_moe_prv_lin_bias_kernel(tc, uT, wu, w, b, gate, offs, pos1, pos2, pos3,
                 return placed.tile(shape, F32, name=name, offset=REGIONS[name], align_bytes=64)
             return keep.tile(shape, F32, name=name, tag=name, align_bytes=64)
 
-        def follower(region, at, name, width):
-            return placed.tile([P, width], U32, name=name, offset=REGIONS[region] + at, align_bytes=64)
+        def follower(region, at, name, width, dtype=U32):
+            return placed.tile([P, width], dtype, name=name, offset=REGIONS[region] + at, align_bytes=64)
 
         def load(name, src, width):
             raw = raw_tile(name, [P, PACK, width])
@@ -69,8 +68,7 @@ def tile_moe_prv_lin_bias_kernel(tc, uT, wu, w, b, gate, offs, pos1, pos2, pos3,
         wu_raw, u_raw, w_raw = {}, {}, {}
         for f in range(PASSES):
             wu_raw[f, 0] = load("wu%d0" % f, wu[rows(f), rows(0)], PASS)
-        for n, (f, lo, hi) in enumerate(U_PIECES):
-            u_raw[n] = load("u%d" % n, uT[rows(f), lo:hi], hi - lo)
+            u_raw[f] = load("u%d" % f, uT[rows(f), :], T)
         offs_sb = load_list("offs_sb", offs, S)
         wu_raw[0, 1] = load("wu01", wu[rows(0), rows(1)], PASS)
         wu_raw[1, 1] = load("wu11", wu[rows(1), rows(1)], PASS)
@@ -97,11 +95,10 @@ def tile_moe_prv_lin_bias_kernel(tc, uT, wu, w, b, gate, offs, pos1, pos2, pos3,
 
         u_q = [planes("uq%d" % f, T) for f in range(PASSES)]
         wu_q = {(f, g): planes("wuq%d%d" % (f, g), PASS) for f in range(PASSES) for g in range(PASSES)}
-        w_q = [planes("wq%d" % h, E * PASSES * P) for h in range(2)]
+        w_q = {(h, q): planes("wq%d%d" % (h, q), PASS) for h in range(2) for q in range(PAIRS) if h == 0 or q == PAIRS - 1}
         x_q = {(g, q): planes("xq%d%d" % (g, q), PAIR) for g in range(PASSES) for q in range(PAIRS)}
-        x_words = {(0, u): keep.tile([P, WINDOW], U32, name="x0%d" % u) for u in range(2)}
-        for u in range(2):
-            nc.gpsimd.memset(x_words[0, u][:, T:WINDOW], 0)
+        x_words = {(0, 0): keep.tile([P, WINDOW], U32, name="x00")}
+        nc.gpsimd.memset(x_words[0, 0][:, T:WINDOW], 0)
         y = {}
 
         def on_vector(dst, src):
@@ -127,14 +124,9 @@ def tile_moe_prv_lin_bias_kernel(tc, uT, wu, w, b, gate, offs, pos1, pos2, pos3,
         def quantize_wu(f, g, u, grouped):
             quantize(wu_q[f, g], slice(u * 2 * P, (u + 1) * 2 * P), grouped)
 
-        def cast_u(raw, grouped, shared):
-            dst = grouped.rearrange("p (c i j) -> p c j i", i=4, j=PACK)
-            src = raw[:].rearrange("p j (c i) -> p c j i", i=4)
-            mid = src.shape[1] * 5 // 8 if shared else src.shape[1]
-            on_vector(dst[:, :mid], src[:, :mid])
-            if shared:
-                on_scalar(dst[:, mid:], src[:, mid:])
-            return grouped
+        def cast_u(f, lo, hi, copy, grouped):
+            copy(grouped.rearrange("p (c i j) -> p c j i", i=4, j=PACK),
+                 u_raw[f][:, :, lo:hi].rearrange("p j (c i) -> p c j i", i=4))
 
         def shared_wu(f, g, scalar_copy):
             grouped = [cast_wu(f, g, 0, on_vector, staging()), cast_wu(f, g, 1, scalar_copy, staging())]
@@ -179,7 +171,7 @@ def tile_moe_prv_lin_bias_kernel(tc, uT, wu, w, b, gate, offs, pos1, pos2, pos3,
                       w_raw[e][:, :, :, h * P:(h + 1) * P].rearrange("p g j (c i) -> p g c j i", i=4))
 
         def quantize_w(q, h, grouped):
-            quantize(w_q[h], slice(q * PASS, (q + 1) * PASS), grouped)
+            quantize(w_q[h, q], slice(0, PASS), grouped)
 
         def experts(q, h):
             banks = [psum.tile([P, C], F32, name="bank") for i in range(2)]
@@ -187,9 +179,9 @@ def tile_moe_prv_lin_bias_kernel(tc, uT, wu, w, b, gate, offs, pos1, pos2, pos3,
                 for i in range(2):
                     e = 2 * q + i
                     cols = slice(i * C, (i + 1) * C)
-                    wcols = slice((e * PASSES + g) * P, (e * PASSES + g + 1) * P)
-                    nc.tensor.matmul_mx(out=banks[i][:], lhsT=w_q[h][0][:, wcols].bitcast(FP8X4),
-                                        lhsT_scale=w_q[h][1][:, wcols],
+                    wcols = slice((i * PASSES + g) * P, (i * PASSES + g + 1) * P)
+                    nc.tensor.matmul_mx(out=banks[i][:], lhsT=w_q[h, q][0][:, wcols].bitcast(FP8X4),
+                                        lhsT_scale=w_q[h, q][1][:, wcols],
                                         rhs=x_q[g, q][0][:, cols].bitcast(FP8X4), rhs_scale=x_q[g, q][1][:, cols],
                                         start=(g == 0), stop=(g == PASSES - 1))
             for i in range(2):
@@ -237,23 +229,32 @@ def tile_moe_prv_lin_bias_kernel(tc, uT, wu, w, b, gate, offs, pos1, pos2, pos3,
                 nc.sync.dma_start(out=out[h * P:(h + 1) * P, halves[n]], in_=total[:, halves[n]])
 
         shared_wu(0, 0, on_scalar_activation)
+        grouped = stage.tile([P, T * PACK], BF16, name="grouped_u", tag="wide", align_bytes=64, bufs=3)
+        cast_u(0, 0, 320, on_vector, grouped[:, :320 * PACK])
+        cast_u(0, 320, T, on_scalar, grouped[:, 320 * PACK:])
+        quantize(u_q[0], slice(0, T), grouped[:])
         shared_wu(1, 0, on_scalar)
-        for n, (f, lo, hi) in enumerate(U_PIECES):
-            grouped = stage.tile([P, (hi - lo) * PACK], BF16, name="grouped_u", tag="wide", align_bytes=64, bufs=3)
-            quantize(u_q[f], slice(lo, hi), cast_u(u_raw[n], grouped[:], hi - lo == HALF))
-        project(0, 0, 0, HALF, on_scalar)
-        project(0, 0, HALF, T - QUARTER, on_scalar)
+        quarters = [staging()[:, :QUARTER * PACK] for n in range(4)]
+        for n in range(4):
+            cast_u(1, n * QUARTER, (n + 1) * QUARTER, (on_vector, on_scalar)[n % 2], quarters[n])
+        for n in range(4):
+            quantize(u_q[1], slice(n * QUARTER, (n + 1) * QUARTER), quarters[n])
+        for n in range(3):
+            project(0, 0, n * QUARTER, (n + 1) * QUARTER, on_vector)
         project(0, 0, T - QUARTER, T, on_vector, "first", 1)
+        for u in range(2):
+            quantize_wu(0, 1, u, cast_wu(0, 1, u, on_scalar, staging()))
+        x_words[0, 1] = follower("wu01", 0, "x01", WINDOW)
+        nc.gpsimd.memset(x_words[0, 1][:, T:WINDOW], 0)
         project(0, 1, HALF, T, on_scalar)
         project(0, 1, 0, HALF, on_scalar, "first", 1)
-        for f in range(PASSES):
-            for u in range(2):
-                quantize_wu(f, 1, u, cast_wu(f, 1, u, on_scalar, staging()))
+        for u in range(2):
+            quantize_wu(1, 1, u, cast_wu(1, 1, u, on_scalar, staging()))
         low = [keep.tile([P, 2 * PASSES * PASS], BF16, name="low%d" % q, align_bytes=64)[:] for q in range(PAIRS)]
         high = [stage.tile([P, 2 * PASSES * PASS], BF16, name="high", tag="wide", align_bytes=64, bufs=3)[:]
                 for q in range(PAIRS)]
-        picked = [gather(0, q, unit("picked")) for q in range(PAIRS)]
-        woven = [weave(picked[q], follower("wu11", q * UNIT_BYTES, "woven0%d" % q, 2 * PAIR)[:], ("vector", "vector")[q])
+        picked = [gather(0, q, unit("picked")) for q in range(2)]
+        woven = [weave(picked[q], follower("wu11", q * UNIT_BYTES - 2048, "woven0%d" % q, 2 * PAIR)[:], ("vector", "vector")[q])
                  for q in range(2)]
         for e, h in ((0, 0), (0, 1), (1, 0)):
             cast_w(e, h, (low, high)[h][e // 2])
@@ -263,20 +264,24 @@ def tile_moe_prv_lin_bias_kernel(tc, uT, wu, w, b, gate, offs, pos1, pos2, pos3,
             for h in range(2):
                 project(1, u, h * HALF, (h + 1) * HALF, on_scalar)
         quantize_x(0, 0, woven[0])
+        picked.append(gather(0, 2, follower("wu11", 2 * UNIT_BYTES - 2048, "picked02", 2 * PAIR)[:]))
         quantize_x(0, 1, woven[1])
         quantize_x(0, 2, weave(picked[2], follower("w0", 2 * WINDOW * 4, "woven02", 2 * PAIR)[:], "scalar"))
         quantize_w(0, 0, low[0])
         picked = [gather(1, q, unit("picked")) for q in range(2)]
         quantize_x(1, 0, weave(picked[0], unit("woven"), "vector"))
-        for e, h in ((2, 0), (3, 0), (3, 1), (4, 0), (5, 0), (1, 1), (5, 1), (2, 1), (4, 1)):
+        for e, h in ((2, 0), (3, 0), (3, 1), (4, 0), (5, 0), (4, 1), (5, 1), (1, 1), (2, 1)):
             cast_w(e, h, (low, high)[h][e // 2])
         quantize_w(1, 0, low[1])
         quantize_x(1, 1, weave(picked[1], follower("w3", 0, "woven11", 2 * PAIR)[:]))
         last = gather(1, 2, follower("w3", UNIT_BYTES, "picked12", 2 * PAIR)[:])
         quantize_w(2, 0, low[2])
-        quantize_x(1, 2, weave(last, keep.tile([P, 2 * PAIR], U32, name="woven12", tag="w1", align_bytes=64)[:]))
-        y[0] = keep.tile([P, S], F32, name="y0", tag="w2", align_bytes=64)
+        quantize_x(1, 2, weave(last, follower("w5", -2048, "woven12", 2 * PAIR)[:]))
+        y[0] = follower("w5", 2048, "y0", S, F32)
         y[1] = keep.tile([P, S], F32, name="y1", tag="w4", align_bytes=64)
+        for q in range(PAIRS - 1):
+            w_q[1, q] = (follower("w5", (q - 1) * 2048, "wq1%dc" % q, PASS),
+                         keep.tile([P, PASS], U8, name="wq1%ds" % q, align_bytes=64))
         for q in range(PAIRS):
             experts(q, 0)
         for q in range(PAIRS):

@@ -254,7 +254,7 @@ def tile_moe_prv_lin_bias_kernel(tc, uT, wu, w, b, gate, offs, pos1, pos2, pos3,
         high = [stage.tile([P, 2 * PASSES * PASS], BF16, name="high", tag="wide", align_bytes=64, bufs=3)[:]
                 for q in range(PAIRS)]
         picked = [gather(0, q, unit("picked")) for q in range(2)]
-        woven = [weave(picked[q], follower("wu11", q * UNIT_BYTES - 2048, "woven0%d" % q, 2 * PAIR)[:], ("vector", "vector")[q])
+        woven = [weave(picked[q], follower("wu11", q * UNIT_BYTES - 2048, "woven0%d" % q, 2 * PAIR)[:], ("scalar", "vector")[q])
                  for q in range(2)]
         for e, h in ((0, 0), (0, 1), (1, 0)):
             cast_w(e, h, (low, high)[h][e // 2])

from contextlib import ExitStack

import concourse.mybir as mybir
from concourse.masks import make_identity

M, K, T, E, C, N, TOP = 1024, 1024, 512, 6, 256, 256, 3
S = E * C
FLOPS = 2 * M * K * T + 2 * K * N * S
BYTES = 4 * (M * T + M * K + E * K * N + N * E + TOP * T + N * T) + 2 * (S + TOP * T)

F32 = mybir.dt.float32
BF16 = mybir.dt.bfloat16
I32 = mybir.dt.int32
U32 = mybir.dt.uint32
U16 = mybir.dt.uint16
U8 = mybir.dt.uint8
FP8X4 = mybir.dt.float8_e4m3fn_x4
MULT = mybir.AluOpType.mult
ADD = mybir.AluOpType.add
COPY = mybir.ActivationFunctionType.Copy
IDENTITY = mybir.ActivationFunctionType.Identity

P = 128
PACK = 4
PASS = P * PACK
PASSES = 2
HALF = T // 2
PAIR = 2 * C
PAIRS = E // 2
QUARTER = T // 4
WINDOW = 704
UNIT_BYTES = 4096
REGIONS = {"wu11": 2048, "w3": 12288, "w0": 20480, "wu01": 30720, "w5": 40960}
PER_COL = 16


def tile_moe_prv_lin_bias_kernel(tc, uT, wu, w, b, gate, offs, pos1, pos2, pos3, out):
    nc = tc.nc
    with ExitStack() as ctx:
        lists = ctx.enter_context(tc.tile_pool(name="lists", bufs=1))
        keep = ctx.enter_context(tc.tile_pool(name="keep", bufs=1))
        placed = ctx.enter_context(tc.tile_pool(name="placed", bufs=1))
        stage = ctx.enter_context(tc.tile_pool(name="stage", bufs=4))
        slots = ctx.enter_context(tc.tile_pool(name="slots", bufs=2))
        psum = ctx.enter_context(tc.psum_pool(name="psum", bufs=6))

        def rows(g):
            return slice(g * PASS, (g + 1) * PASS)

        def raw_tile(name, shape):
            if name in REGIONS:
                return placed.tile(shape, F32, name=name, offset=REGIONS[name], align_bytes=64)
            return keep.tile(shape, F32, name=name, tag=name, align_bytes=64)

        def follower(region, at, name, width, dtype=U32):
            return placed.tile([P, width], dtype, name=name, offset=REGIONS[region] + at, align_bytes=64)

        def load(name, src, width):
            raw = raw_tile(name, [P, PACK, width])
            nc.sync.dma_start(out=raw[:], in_=src.rearrange("(p j) c -> p j c", j=PACK))
            return raw

        def load_list(name, src, n):
            held = lists.tile([P, n // PER_COL], U16, name=name)
            nc.sync.dma_start(held[:], src)
            return held

        wu_raw, u_raw, w_raw = {}, {}, {}
        for f in range(PASSES):
            wu_raw[f, 0] = load("wu%d0" % f, wu[rows(f), rows(0)], PASS)
            u_raw[f] = load("u%d" % f, uT[rows(f), :], T)
        offs_sb = load_list("offs_sb", offs, S)
        wu_raw[0, 1] = load("wu01", wu[rows(0), rows(1)], PASS)
        wu_raw[1, 1] = load("wu11", wu[rows(1), rows(1)], PASS)
        for e in range(E):
            w_raw[e] = raw_tile("w%d" % e, [P, PASSES, PACK, N])
            nc.sync.dma_start(out=w_raw[e][:], in_=w[e].rearrange("(g p j) n -> p g j n", g=PASSES, j=PACK))
        bias = keep.tile([P, 2, E], F32, name="bias", tag="bias", align_bytes=64)
        nc.sync.dma_start(out=bias[:], in_=b.rearrange("(h p) e -> p h e", p=P))
        gate_rows = keep.tile([P, TOP, T], F32, name="gate_rows")
        nc.sync.dma_start(out=gate_rows[:], in_=gate[:, 0:P, :].rearrange("r p t -> p r t"))
        pos_sb = [load_list("pos%d" % r, src, T) for r, src in enumerate((pos1, pos2, pos3))]
        gate_cols = []
        for r in range(TOP):
            column = keep.tile([P, T // P], F32, name="gate_col%d" % r)
            with nc.allow_non_contiguous_dma(reason="one gate value for each partition"):
                nc.sync.dma_start(out=column[:], in_=gate[r, 0, :].rearrange("(c p) -> p c", p=P))
            gate_cols.append(column)
        identity = keep.tile([P, P], F32, name="identity")
        make_identity(nc, identity[:])

        def planes(name, width):
            return (keep.tile([P, width], U32, name=name + "c", align_bytes=64),
                    keep.tile([P, width], U8, name=name + "s", align_bytes=64))

        u_q = [planes("uq%d" % f, T) for f in range(PASSES)]
        wu_q = {(f, g): planes("wuq%d%d" % (f, g), PASS) for f in range(PASSES) for g in range(PASSES)}
        w_q = {(h, q): planes("wq%d%d" % (h, q), PASS) for h in range(2) for q in range(PAIRS) if h == 0 or q == PAIRS - 1}
        x_q = {(g, q): planes("xq%d%d" % (g, q), PAIR) for g in range(PASSES) for q in range(PAIRS)}
        x_words = {(0, 0): keep.tile([P, WINDOW], U32, name="x00")}
        nc.gpsimd.memset(x_words[0, 0][:, T:WINDOW], 0)
        y = {}

        def on_vector(dst, src):
            nc.vector.tensor_copy(out=dst, in_=src)

        def on_scalar(dst, src):
            nc.scalar.copy(out=dst, in_=src)

        def on_scalar_activation(dst, src):
            nc.scalar.activation(out=dst, in_=src, func=IDENTITY)

        def quantize(q, cols, grouped):
            nc.vector.quantize_mx(out=q[0][:, cols].bitcast(FP8X4), scales=q[1][:, cols], in_=grouped)

        def cast_wu(f, g, u, copy, grouped):
            copy(grouped.rearrange("p (e m j) -> p m j e", e=2, j=PACK),
                 wu_raw[f, g][:].rearrange("p j (m t) -> p m j t", t=PACK)[:, :, :, 2 * u:2 * u + 2])
            return grouped

        def staging():
            return stage.tile([P, 2 * P * PACK], BF16, name="grouped", tag="grouped", align_bytes=64)[:]

        def quantize_wu(f, g, u, grouped):
            quantize(wu_q[f, g], slice(u * 2 * P, (u + 1) * 2 * P), grouped)

        def cast_u(f, lo, hi, copy, grouped):
            copy(grouped.rearrange("p (c i j) -> p c j i", i=4, j=PACK),
                 u_raw[f][:, :, lo:hi].rearrange("p j (c i) -> p c j i", i=4))

        def shared_wu(f, g, scalar_copy):
            grouped = [cast_wu(f, g, 0, on_vector, staging()), cast_wu(f, g, 1, scalar_copy, staging())]
            for u in range(2):
                quantize_wu(f, g, u, grouped[u])

        def project(g, u, lo, hi, copy, tag="bank", bufs=6):
            bank = psum.tile([P, 2, hi - lo], F32, name="bank", tag=tag, bufs=bufs)
            tokens = slice(lo, hi)
            for e in range(2):
                cols = slice((2 * u + e) * P, (2 * u + e + 1) * P)
                for f in range(PASSES):
                    nc.tensor.matmul_mx(out=bank[:, e, :], lhsT=wu_q[f, g][0][:, cols].bitcast(FP8X4),
                                        lhsT_scale=wu_q[f, g][1][:, cols],
                                        rhs=u_q[f][0][:, tokens].bitcast(FP8X4), rhs_scale=u_q[f][1][:, tokens],
                                        start=(f == 0), stop=(f == PASSES - 1))
            pairs = x_words[g, u][:, tokens].bitcast(BF16).rearrange("p (c e) -> p c e", e=2)
            copy(pairs, bank[:].rearrange("p e c -> p c e"))

        def unit(tag):
            return slots.tile([P, 2 * PAIR], U32, name=tag, tag=tag, align_bytes=64)[:]

        def gather(g, q, picked):
            cols = slice(q * PAIR // PER_COL, (q + 1) * PAIR // PER_COL)
            for u in range(2):
                nc.vector.tensor_copy(out=picked[:, u * PAIR:(u + 1) * PAIR],
                                      in_=x_words[g, u][:].indirect(offs_sb[:, cols]))
            return picked

        def weave(picked, woven, engine="vector"):
            view = I32 if engine == "vector" else U32
            dst = woven.bitcast(view).rearrange("p (c i u) -> p c u i", i=2, u=2)
            src = picked.bitcast(view).rearrange("p (u c i) -> p c u i", u=2, i=2)
            (on_vector if engine == "vector" else on_scalar)(dst, src)
            return woven

        def quantize_x(g, q, woven):
            quantize(x_q[g, q], slice(0, PAIR), woven.bitcast(BF16))

        def cast_w(e, h, grouped):
            on_scalar(grouped[:, (e % 2) * PASSES * PASS:(e % 2 + 1) * PASSES * PASS].rearrange("p (g c i j) -> p g c j i", g=PASSES, i=4, j=PACK),
                      w_raw[e][:, :, :, h * P:(h + 1) * P].rearrange("p g j (c i) -> p g c j i", i=4))

        def quantize_w(q, h, grouped):
            quantize(w_q[h, q], slice(0, PASS), grouped)

        def experts(q, h):
            banks = [psum.tile([P, C], F32, name="bank") for i in range(2)]
            for g in range(PASSES):
                for i in range(2):
                    e = 2 * q + i
                    cols = slice(i * C, (i + 1) * C)
                    wcols = slice((i * PASSES + g) * P, (i * PASSES + g + 1) * P)
                    nc.tensor.matmul_mx(out=banks[i][:], lhsT=w_q[h, q][0][:, wcols].bitcast(FP8X4),
                                        lhsT_scale=w_q[h, q][1][:, wcols],
                                        rhs=x_q[g, q][0][:, cols].bitcast(FP8X4), rhs_scale=x_q[g, q][1][:, cols],
                                        start=(g == 0), stop=(g == PASSES - 1))
            for i in range(2):
                e = 2 * q + i
                nc.scalar.activation(out=y[h][:, e * C:(e + 1) * C], in_=banks[i][:], func=IDENTITY,
                                     bias=bias[:, h, e:e + 1])

        def combine_turned(h):
            scaled = keep.tile([P, TOP, T], F32, name="scaled", tag="wu00", align_bytes=64)
            for r in range(TOP):
                fetched = stage.tile([P, T], F32, name="fetched", tag="grouped", align_bytes=64)
                nc.vector.tensor_copy(out=fetched[:], in_=y[h][:].indirect(pos_sb[r][:]))
                bank = psum.tile([P, T], F32, name="bank")
                for c in range(T // P):
                    cols = slice(c * P, (c + 1) * P)
                    nc.tensor.transpose(bank[:, cols], fetched[:, cols], identity[:])
                for c in range(T // P):
                    cols = slice(c * P, (c + 1) * P)
                    nc.scalar.activation(out=scaled[:, r, cols], in_=bank[:, cols], func=COPY,
                                         scale=gate_cols[r][:, c:c + 1])
            summed = psum.tile([P, T], F32, name="bank")
            for c in range(T // P):
                cols = slice(c * P, (c + 1) * P)
                for r in range(TOP):
                    nc.tensor.matmul(summed[:, cols], scaled[:, r, cols], identity[:], is_transpose=True,
                                     start=(r == 0), stop=(r == TOP - 1))
            total = keep.tile([P, T], F32, name="total%d" % h)
            on_scalar(total[:], summed[:])
            nc.scalar.dma_start(out=out[h * P:(h + 1) * P, :], in_=total[:])

        def combine_fused(h):
            terms = keep.tile([P, TOP * T], F32, name="terms", tag="wu10", align_bytes=64)
            for r in range(TOP):
                nc.vector.tensor_tensor(terms[:, r * T:(r + 1) * T], y[h][:].indirect(pos_sb[r][:]),
                                        gate_rows[:, r, :], MULT)
            partial = keep.tile([P, T], F32, name="partial")
            total = keep.tile([P, T], F32, name="total%d" % h)
            halves = [slice(n * HALF, (n + 1) * HALF) for n in range(2)]
            for n in range(2):
                nc.vector.tensor_tensor(partial[:, halves[n]], terms[:, n * HALF:(n + 1) * HALF],
                                        terms[:, T + n * HALF:T + (n + 1) * HALF], ADD)
            for n in range(2):
                nc.vector.tensor_tensor(total[:, halves[n]], partial[:, halves[n]],
                                        terms[:, 2 * T + n * HALF:2 * T + (n + 1) * HALF], ADD)
                nc.sync.dma_start(out=out[h * P:(h + 1) * P, halves[n]], in_=total[:, halves[n]])

        shared_wu(0, 0, on_scalar_activation)
        grouped = stage.tile([P, T * PACK], BF16, name="grouped_u", tag="wide", align_bytes=64, bufs=3)
        cast_u(0, 0, 320, on_vector, grouped[:, :320 * PACK])
        cast_u(0, 320, T, on_scalar, grouped[:, 320 * PACK:])
        quantize(u_q[0], slice(0, T), grouped[:])
        shared_wu(1, 0, on_scalar)
        quarters = [staging()[:, :QUARTER * PACK] for n in range(4)]
        for n in range(4):
            cast_u(1, n * QUARTER, (n + 1) * QUARTER, (on_vector, on_scalar)[n % 2], quarters[n])
        for n in range(4):
            quantize(u_q[1], slice(n * QUARTER, (n + 1) * QUARTER), quarters[n])
        for n in range(3):
            project(0, 0, n * QUARTER, (n + 1) * QUARTER, on_vector)
        project(0, 0, T - QUARTER, T, on_vector, "first", 1)
        for u in range(2):
            quantize_wu(0, 1, u, cast_wu(0, 1, u, on_scalar, staging()))
        x_words[0, 1] = follower("wu01", 0, "x01", WINDOW)
        nc.gpsimd.memset(x_words[0, 1][:, T:WINDOW], 0)
        project(0, 1, HALF, T, on_scalar)
        project(0, 1, 0, HALF, on_scalar, "first", 1)
        for u in range(2):
            quantize_wu(1, 1, u, cast_wu(1, 1, u, on_scalar, staging()))
        low = [keep.tile([P, 2 * PASSES * PASS], BF16, name="low%d" % q, align_bytes=64)[:] for q in range(PAIRS)]
        high = [stage.tile([P, 2 * PASSES * PASS], BF16, name="high", tag="wide", align_bytes=64, bufs=3)[:]
                for q in range(PAIRS)]
        picked = [gather(0, q, unit("picked")) for q in range(2)]
        woven = [weave(picked[q], follower("wu11", q * UNIT_BYTES - 2048, "woven0%d" % q, 2 * PAIR)[:], ("scalar", "vector")[q])
                 for q in range(2)]
        for e, h in ((0, 0), (0, 1), (1, 0)):
            cast_w(e, h, (low, high)[h][e // 2])
        for u in range(2):
            x_words[1, u] = follower("w0", u * WINDOW * 4, "x1%d" % u, WINDOW)
            nc.gpsimd.memset(x_words[1, u][:, T:WINDOW], 0)
            for h in range(2):
                project(1, u, h * HALF, (h + 1) * HALF, on_scalar)
        quantize_x(0, 0, woven[0])
        picked.append(gather(0, 2, follower("wu11", 2 * UNIT_BYTES - 2048, "picked02", 2 * PAIR)[:]))
        quantize_x(0, 1, woven[1])
        quantize_x(0, 2, weave(picked[2], follower("w0", 2 * WINDOW * 4, "woven02", 2 * PAIR)[:], "scalar"))
        quantize_w(0, 0, low[0])
        picked = [gather(1, q, unit("picked")) for q in range(2)]
        quantize_x(1, 0, weave(picked[0], unit("woven"), "vector"))
        for e, h in ((2, 0), (3, 0), (3, 1), (4, 0), (5, 0), (4, 1), (5, 1), (1, 1), (2, 1)):
            cast_w(e, h, (low, high)[h][e // 2])
        quantize_w(1, 0, low[1])
        quantize_x(1, 1, weave(picked[1], follower("w3", 0, "woven11", 2 * PAIR)[:]))
        last = gather(1, 2, follower("w3", UNIT_BYTES, "picked12", 2 * PAIR)[:])
        quantize_w(2, 0, low[2])
        quantize_x(1, 2, weave(last, follower("w5", -2048, "woven12", 2 * PAIR)[:]))
        y[0] = follower("w5", 2048, "y0", S, F32)
        y[1] = keep.tile([P, S], F32, name="y1", tag="w4", align_bytes=64)
        for q in range(PAIRS - 1):
            w_q[1, q] = (follower("w5", (q - 1) * 2048, "wq1%dc" % q, PASS),
                         keep.tile([P, PASS], U8, name="wq1%ds" % q, align_bytes=64))
        for q in range(PAIRS):
            experts(q, 0)
        for q in range(PAIRS):
            quantize_w(q, 1, high[q])
            experts(q, 1)
        combine_turned(0)
        combine_fused(1)
